import numpy as np
CORES = [0,8,16,24,32,40,48,56,64,72,80,88,96,104,112,120]
N = 16
GROUPS = [[0,2,4,6,8,10,12,14],[1,3,5,7,9,11,13,15]]
def setup_inputs(rng):
    return {"x": rng.standard_normal((N, 128, 64), dtype=np.float32)}
def reference(x):
    y = np.empty((N, 128, 64), x.dtype)
    for g in GROUPS:
        n = len(g); b = x.shape[2] // n
        for i, r in enumerate(g):
            y[r] = np.concatenate([x[s][:, i * b:(i + 1) * b] for s in g], axis=1)
    return {"y": y}

@@ -1,0 +1,38 @@
+import concourse.bass as bass
+
+SCRATCH = {
+    "xs": ("sbuf", [128, 64], "float32"),
+    "land": ("sbuf", [128, 64], "float32"),
+}
+SEMAPHORES = ["loaded", "arrived", "stored"]
+
+
+def rank_program(g, core, T, topo):
+    rank = T.rank_of(core)
+    if rank is None:
+        return
+    group = [grp for grp in T.tables["GROUPS"] if rank in grp][0]
+    n = len(group)
+    me = group.index(rank)
+    b = T.x.shape[1] // n
+
+    def blk(j):
+        return slice(j * b, (j + 1) * b)
+
+    g.dma_start(T.xs[:], T.x[:]).then_inc(T.sem.loaded, 16)
+    g.wait_ge(T.sem.loaded, 16)
+
+    transfers = []
+    for e, j in enumerate([(me + d) % n for d in range(1, n)]):
+        a = topo.addr(T.cores[group[j]])
+        transfers.append(bass.RemoteDMATransfer(
+            dst_ids=[bass.DstId(rid=a[0], pnc=a[1])], dma_engine_mask=1 << e, remote_sem=T.sem.arrived,
+            src=T.xs[:, blk(j)], dst=T.land[:, blk(me)]))
+    g.remote_dma_fused(transfers, local_sem=T.sem.arrived)
+
+    g.dma_start(T.land[:, blk(me)], T.x[:, blk(me)]).then_inc(T.sem.loaded, 16)
+
+    g.wait_ge(T.sem.arrived, 2 * (n - 1))
+    g.wait_ge(T.sem.loaded, 32)
+    g.dma_start(T.y[:], T.land[:]).then_inc(T.sem.stored, 16)
+    g.wait_ge(T.sem.stored, 16)

@@ -4,7 +4,7 @@ SCRATCH = {
     "xs": ("sbuf", [128, 64], "float32"),
     "land": ("sbuf", [128, 64], "float32"),
 }
-SEMAPHORES = ["loaded", "arrived", "stored"]
+SEMAPHORES = ["loaded", "own", "arrived", "stored"]
 
 
 def rank_program(g, core, T, topo):
@@ -20,6 +20,7 @@ def rank_program(g, core, T, topo):
         return slice(j * b, (j + 1) * b)
 
     g.dma_start(T.xs[:], T.x[:]).then_inc(T.sem.loaded, 16)
+    g.dma_start(T.land[:, blk(me)], T.x[:, blk(me)]).then_inc(T.sem.own, 16)
     g.wait_ge(T.sem.loaded, 16)
 
     transfers = []
@@ -30,9 +31,7 @@ def rank_program(g, core, T, topo):
             src=T.xs[:, blk(j)], dst=T.land[:, blk(me)]))
     g.remote_dma_fused(transfers, local_sem=T.sem.arrived)
 
-    g.dma_start(T.land[:, blk(me)], T.x[:, blk(me)]).then_inc(T.sem.loaded, 16)
-
+    g.wait_ge(T.sem.own, 16)
     g.wait_ge(T.sem.arrived, 2 * (n - 1))
-    g.wait_ge(T.sem.loaded, 32)
     g.dma_start(T.y[:], T.land[:]).then_inc(T.sem.stored, 16)
     g.wait_ge(T.sem.stored, 16)

import concourse.bass as bass

SCRATCH = {
    "xs": ("sbuf", [128, 64], "float32"),
    "land": ("sbuf", [128, 64], "float32"),
}
SEMAPHORES = ["loaded", "own", "arrived", "stored"]


def rank_program(g, core, T, topo):
    rank = T.rank_of(core)
    if rank is None:
        return
    group = [grp for grp in T.tables["GROUPS"] if rank in grp][0]
    n = len(group)
    me = group.index(rank)
    b = T.x.shape[1] // n

    def blk(j):
        return slice(j * b, (j + 1) * b)

    g.dma_start(T.xs[:], T.x[:]).then_inc(T.sem.loaded, 16)
    g.dma_start(T.land[:, blk(me)], T.x[:, blk(me)]).then_inc(T.sem.own, 16)
    g.wait_ge(T.sem.loaded, 16)

    transfers = []
    for e, j in enumerate([(me + d) % n for d in range(1, n)]):
        a = topo.addr(T.cores[group[j]])
        transfers.append(bass.RemoteDMATransfer(
            dst_ids=[bass.DstId(rid=a[0], pnc=a[1])], dma_engine_mask=1 << e, remote_sem=T.sem.arrived,
            src=T.xs[:, blk(j)], dst=T.land[:, blk(me)]))
    g.remote_dma_fused(transfers, local_sem=T.sem.arrived)

    g.wait_ge(T.sem.own, 16)
    g.wait_ge(T.sem.arrived, 2 * (n - 1))
    g.dma_start(T.y[:], T.land[:]).then_inc(T.sem.stored, 16)
    g.wait_ge(T.sem.stored, 16)
